import numpy as np
import ml_dtypes


def mxq(x, axis, fmt="e4m3"):
    dtype, down = {"e4m3": (ml_dtypes.float8_e4m3fn, 7), "e5m2": (ml_dtypes.float8_e5m2, 14)}[fmt]
    v = np.moveaxis(np.asarray(x, np.float32).astype(ml_dtypes.bfloat16).astype(np.float64), axis, -1)
    blocks = v.reshape(v.shape[:-1] + (-1, 32))
    amax = np.abs(blocks).max(-1, keepdims=True)
    byte = np.maximum(np.where(amax > 0, np.frexp(amax)[1] - 1 + 127, 0) - down, 1)
    scale = np.exp2(byte - 127.0)
    codes = (blocks / scale).astype(np.float32).astype(dtype).astype(np.float64)
    return np.moveaxis((codes * scale).reshape(v.shape), -1, axis)


WIDE = False


def mx_kscale(k):
    if not WIDE:
        return np.ones(k)
    levels = np.array([10, -10, 5, -5, 0])
    if k % 512:
        return np.exp2(np.random.permutation(np.resize(levels, k // 32))).repeat(32)
    a = np.empty((k // 512, 16))
    for p in range(k // 512):
        a[p, :8] = np.random.permutation(np.resize(levels, 8))
        for g in range(8):
            far = levels[np.abs(levels - a[p, g]) >= 10]
            a[p, g + 8] = far[np.random.randint(len(far))]
    return np.exp2(a.ravel()).repeat(32)


def f64(x):
    return np.asarray(x).astype(np.float64)


def striped8(idx):
    return np.asarray(idx).reshape(8, -1, 16).transpose(0, 2, 1).reshape(128, -1).astype(np.uint16)


def unstriped8(offs):
    return offs.reshape(8, 16, -1).transpose(0, 2, 1).reshape(8, -1).astype(np.int64)


def pick8(x, idx, run):
    r = np.arange(len(x))
    return x[r[:, None], idx[r % (8 * run) // run]]


E2M1 = np.array([0.0, 0.5, 1.0, 1.5, 2.0, 3.0, 4.0, 6.0, -0.0, -0.5, -1.0, -1.5, -2.0, -3.0, -4.0, -6.0])


def pack_weight(w, fmt):
    k, n = w.shape
    w = f64(np.asarray(w, np.float32).astype(ml_dtypes.bfloat16)).reshape(k // 32, 32, n)
    amax = np.abs(w).max(1)
    if fmt == "e4m3":
        byte = np.frexp(amax)[1] - 1 + 127 - 7
    else:
        mant, ex = np.frexp(amax / 6.0)
        byte = np.where(mant > 0.5, ex, ex - 1) + 127
    byte = np.clip(np.where(amax > 0, byte, 1), 1, 254)
    scaled = (w * np.exp2(127.0 - byte)[:, None, :]).reshape(k, n).astype(np.float32)
    by_word = np.ascontiguousarray(scaled.reshape(k // 512, 128, 4, n).transpose(0, 1, 3, 2))
    if fmt == "e4m3":
        words = by_word.astype(ml_dtypes.float8_e4m3fn).view(np.uint8)
    else:
        c = by_word.astype(ml_dtypes.float4_e2m1fn).view(np.uint8) & 0xF
        words = (c[..., 0::2] | (c[..., 1::2] << 4)).reshape(k // 512, 128, 2 * n)
    return np.ascontiguousarray(words), np.ascontiguousarray(byte.astype(np.uint8).reshape(k // 512, 16, n))


def unpack_weight(words, scales, fmt):
    g, _, n = scales.shape
    words = np.ascontiguousarray(words).reshape(g, 128, n, -1)
    if fmt == "e4m3":
        vals = words.view(ml_dtypes.float8_e4m3fn).astype(np.float64)
    else:
        nib = np.empty((g, 128, n, 4), np.uint8)
        nib[..., 0::2] = words & 0xF
        nib[..., 1::2] = words >> 4
        vals = E2M1[nib]
    vals = vals * np.repeat(np.exp2(scales.astype(np.float64) - 127.0), 8, axis=1)[..., None]
    return vals.transpose(0, 1, 3, 2).reshape(g * 512, n)


D, T, U, I, Q = 512, 1024, 1024, 512, 128


def setup_inputs():
    n = np.random.standard_normal
    idx = np.stack([np.random.permutation(T)[:I] for _ in range(8)])
    idx2 = np.stack([np.random.permutation(U)[:I] for _ in range(8)])
    idx3 = np.stack([np.random.permutation(I)[:I] for _ in range(8)])
    idx4 = np.stack([np.random.permutation(T)[:I] for _ in range(8)])
    idx5 = np.stack([np.random.permutation(T)[:I] for _ in range(8)])
    fd = mx_kscale(D)
    keysp = pack_weight(n((D, T)) / fd[:, None], "e2m1")
    notesp = pack_weight(n((D, U)) / fd[:, None], "e4m3")
    return {
        "query": (n((D, Q)) * 1.0 / np.sqrt(D) * fd[:, None]).astype(np.float32),
        "keys_words": keysp[0],
        "keys_scales": keysp[1],
        "notes_words": notesp[0],
        "notes_scales": notesp[1],
        "offs": striped8(idx),
        "offs2": striped8(idx2),
        "offs3": striped8(idx3),
        "offs4": striped8(idx4),
        "offs5": striped8(idx5),
    }


def reference(query, keys_words, keys_scales, notes_words, notes_scales, offs, offs2, offs3, offs4, offs5):
    idx = unstriped8(offs)
    idx2 = unstriped8(offs2)
    idx3 = unstriped8(offs3)
    idx4 = unstriped8(offs4)
    idx5 = unstriped8(offs5)
    keysu = unpack_weight(keys_words, keys_scales, "e2m1")
    notesu = unpack_weight(notes_words, notes_scales, "e4m3")
    queryq = mxq(f64(query), 0, "e4m3")
    a = queryq.T @ keysu
    b = queryq.T @ notesu
    r = pick8(a, idx, 16) - pick8(b, idx2, 16)
    v = pick8(r, idx3, 16)
    m1 = np.maximum(r, v)
    f1 = np.zeros((Q, T))
    f1[np.arange(Q)[:, None], idx4[np.arange(Q) % 128 // 16]] = m1
    aa = a - f1
    y = pick8(aa, idx5, 16) + v
    return y

@@ -1,0 +1,128 @@
+from contextlib import ExitStack
+
+import concourse.mybir as mybir
+
+F32 = mybir.dt.float32
+BF16 = mybir.dt.bfloat16
+I32 = mybir.dt.int32
+U32 = mybir.dt.uint32
+U16 = mybir.dt.uint16
+U8 = mybir.dt.uint8
+FP8X4 = mybir.dt.float8_e4m3fn_x4
+FP4X4 = mybir.dt.float4_e2m1fn_x4
+COPY = mybir.ActivationFunctionType.Copy
+ADD = mybir.AluOpType.add
+SUB = mybir.AluOpType.subtract
+MAX = mybir.AluOpType.max
+
+P = 128
+PACK = 4
+D, T, U, SLOTS, Q = 512, 1024, 1024, 512, 128
+GROUP = 16
+N_MM = 256
+HALF = SLOTS // 2
+LEAD = 128
+
+FLOPS = 2 * D * Q * (T + U)
+
+
+def tile_attend_slotrivals_two_kernel(tc, query, keys_words, keys_scales, notes_words, notes_scales,
+                                       offs, offs2, offs3, offs4, offs5, out):
+    nc = tc.nc
+    with ExitStack() as ctx:
+        keep = ctx.enter_context(tc.tile_pool(name="keep", bufs=1))
+        psum = ctx.enter_context(tc.psum_pool(name="psum", bufs=1))
+
+        def entries(lst, lo, hi):
+            return lst[:, lo // GROUP : hi // GROUP]
+
+        note_scale = keep.tile([P, U], U8, name="note_scale", align_bytes=64)
+        key_scale = keep.tile([P, T], U8, name="key_scale", align_bytes=64)
+        f1 = keep.tile([P, T], F32, name="f1")
+        nc.vector.memset(note_scale[:].bitcast(I32), 0)
+        nc.gpsimd.memset(key_scale[:].bitcast(I32), 0)
+        nc.vector.memset(f1[:], 0.0)
+
+        q_raw = keep.tile([P, PACK, Q], F32, name="q_raw")
+        nc.sync.dma_start(out=q_raw[:], in_=query.rearrange("(p j) q -> p j q", j=PACK))
+        for quad in range(4):
+            nc.scalar.dma_start(out=note_scale[32 * quad : 32 * quad + 4, :].bitcast(I32),
+                                in_=notes_scales[0, 4 * quad : 4 * quad + 4, :].bitcast(I32))
+        note_bytes = notes_words[0].rearrange("p c r -> p (c r)")
+        note_code = []
+        for h in range(2):
+            part = keep.tile([P, U // 2], U32, name=f"note_code{h}", align_bytes=64)
+            nc.sync.dma_start(out=part[:].bitcast(I32),
+                              in_=note_bytes[:, h * 2 * U : (h + 1) * 2 * U].bitcast(I32))
+            note_code.append(part)
+        key_code = keep.tile([P, 2 * T], U8, name="key_code", align_bytes=64)
+        nc.sync.dma_start(out=key_code[:].bitcast(I32), in_=keys_words[0].bitcast(I32))
+        for quad in range(4):
+            nc.sync.dma_start(out=key_scale[32 * quad : 32 * quad + 4, :].bitcast(I32),
+                              in_=keys_scales[0, 4 * quad : 4 * quad + 4, :].bitcast(I32))
+        lists = []
+        for name, src in (("idx2", offs2), ("idx", offs), ("idx3", offs3), ("idx4", offs4), ("idx5", offs5)):
+            lst = keep.tile([P, SLOTS // GROUP], U16, name=name)
+            nc.sync.dma_start(lst[:], src)
+            lists.append(lst)
+        idx2, idx, idx3, idx4, idx5 = lists
+
+        q_bf = keep.tile([P, Q, PACK], BF16, name="q_bf", align_bytes=64)
+        nc.vector.tensor_copy(out=q_bf[:].rearrange("p (c i) j -> p c j i", i=4),
+                              in_=q_raw[:].rearrange("p j (c i) -> p c j i", i=4))
+        q_code = keep.tile([P, Q], U32, name="q_code", align_bytes=64)
+        q_scale = keep.tile([P, Q], U8, name="q_scale", align_bytes=64)
+        nc.vector.quantize_mx(out=q_code[:].bitcast(FP8X4), scales=q_scale[:],
+                              in_=q_bf[:].rearrange("p q j -> p (q j)"))
+
+        def score(dst, name, piece, codes, scales):
+            bank = psum.tile([P, N_MM], F32, name=f"{name}_bank{piece}")
+            nc.tensor.matmul_mx(out=bank[:], lhsT=q_code[:].bitcast(FP8X4), lhsT_scale=q_scale[:],
+                                rhs=codes, rhs_scale=scales, start=True, stop=True)
+            cols = dst[:, piece * N_MM : (piece + 1) * N_MM]
+            if piece % 2 == 0:
+                nc.scalar.activation(cols, bank[:], COPY)
+            else:
+                nc.vector.tensor_copy(cols, bank[:])
+
+        b = keep.tile([P, U], F32, name="b")
+        for piece in range(U // N_MM):
+            lo = piece * N_MM
+            part, at = divmod(lo, U // 2)
+            score(b, "b", piece, note_code[part][:, at : at + N_MM].bitcast(FP8X4),
+                  note_scale[:, lo : lo + N_MM])
+        b_at = keep.tile([P, SLOTS], F32, name="b_at")
+        nc.scalar.activation(b_at[:, :HALF], b[:].indirect(entries(idx2, 0, HALF)), COPY)
+        nc.vector.tensor_copy(b_at[:, HALF:], b[:].indirect(entries(idx2, HALF, SLOTS)))
+
+        a = keep.tile([P, T], F32, name="a")
+        for piece in range(T // N_MM):
+            lo = piece * N_MM
+            score(a, "a", piece, key_code[:, 2 * lo : 2 * (lo + N_MM)].bitcast(FP4X4),
+                  key_scale[:, lo : lo + N_MM])
+
+        r = keep.tile([P, SLOTS], F32, name="r")
+        a_at = keep.tile([P, HALF], F32, name="a_at")
+        nc.vector.tensor_tensor(r[:, :HALF], a[:].indirect(entries(idx, 0, HALF)), b_at[:, :HALF], SUB)
+        nc.scalar.activation(a_at[:], a[:].indirect(entries(idx, HALF, SLOTS)), COPY)
+        nc.vector.tensor_tensor(r[:, HALF:], a_at[:], b_at[:, HALF:], SUB)
+
+        v = keep.tile([P, SLOTS], F32, name="v")
+        m1 = keep.tile([P, SLOTS], F32, name="m1")
+        nc.vector.tensor_copy(v[:, :LEAD], r[:].indirect(entries(idx3, 0, LEAD)))
+        nc.scalar.activation(v[:, LEAD:HALF], r[:].indirect(entries(idx3, LEAD, HALF)), COPY)
+        nc.scalar.activation(v[:, HALF:], r[:].indirect(entries(idx3, HALF, SLOTS)), COPY)
+        for lo, hi in ((0, LEAD), (LEAD, SLOTS)):
+            nc.vector.tensor_tensor(m1[:, lo:hi], r[:, lo:hi], v[:, lo:hi], MAX)
+            nc.vector.tensor_copy(f1[:].indirect(entries(idx4, lo, hi)), m1[:, lo:hi])
+
+        aa = keep.tile([P, T], F32, name="aa")
+        nc.vector.tensor_tensor(aa[:], a[:], f1[:], SUB)
+
+        res = keep.tile([P, SLOTS], F32, name="res")
+        aa_at = keep.tile([P, HALF], F32, name="aa_at")
+        nc.vector.tensor_tensor(res[:, :HALF], aa[:].indirect(entries(idx5, 0, HALF)), v[:, :HALF], ADD)
+        nc.scalar.activation(aa_at[:], aa[:].indirect(entries(idx5, HALF, SLOTS)), COPY)
+        nc.sync.dma_start(out=out[:, :HALF], in_=res[:, :HALF])
+        nc.vector.tensor_tensor(res[:, HALF:], aa_at[:], v[:, HALF:], ADD)
+        nc.sync.dma_start(out=out[:, HALF:], in_=res[:, HALF:])

@@ -21,7 +21,6 @@ D, T, U, SLOTS, Q = 512, 1024, 1024, 512, 128
 GROUP = 16
 N_MM = 256
 HALF = SLOTS // 2
-LEAD = 128
 
 FLOPS = 2 * D * Q * (T + U)
 
@@ -40,13 +39,13 @@ def tile_attend_slotrivals_two_kernel(tc, query, keys_words, keys_scales, notes_
         key_scale = keep.tile([P, T], U8, name="key_scale", align_bytes=64)
         f1 = keep.tile([P, T], F32, name="f1")
         nc.vector.memset(note_scale[:].bitcast(I32), 0)
-        nc.gpsimd.memset(key_scale[:].bitcast(I32), 0)
+        nc.vector.memset(key_scale[:].bitcast(I32), 0)
         nc.vector.memset(f1[:], 0.0)
 
         q_raw = keep.tile([P, PACK, Q], F32, name="q_raw")
         nc.sync.dma_start(out=q_raw[:], in_=query.rearrange("(p j) q -> p j q", j=PACK))
         for quad in range(4):
-            nc.scalar.dma_start(out=note_scale[32 * quad : 32 * quad + 4, :].bitcast(I32),
+            nc.sync.dma_start(out=note_scale[32 * quad : 32 * quad + 4, :].bitcast(I32),
                                 in_=notes_scales[0, 4 * quad : 4 * quad + 4, :].bitcast(I32))
         note_bytes = notes_words[0].rearrange("p c r -> p (c r)")
         note_code = []
@@ -75,12 +74,12 @@ def tile_attend_slotrivals_two_kernel(tc, query, keys_words, keys_scales, notes_
         nc.vector.quantize_mx(out=q_code[:].bitcast(FP8X4), scales=q_scale[:],
                               in_=q_bf[:].rearrange("p q j -> p (q j)"))
 
-        def score(dst, name, piece, codes, scales):
+        def score(dst, name, piece, codes, scales, on_scalar):
             bank = psum.tile([P, N_MM], F32, name=f"{name}_bank{piece}")
             nc.tensor.matmul_mx(out=bank[:], lhsT=q_code[:].bitcast(FP8X4), lhsT_scale=q_scale[:],
                                 rhs=codes, rhs_scale=scales, start=True, stop=True)
             cols = dst[:, piece * N_MM : (piece + 1) * N_MM]
-            if piece % 2 == 0:
+            if on_scalar:
                 nc.scalar.activation(cols, bank[:], COPY)
             else:
                 nc.vector.tensor_copy(cols, bank[:])
@@ -90,16 +89,15 @@ def tile_attend_slotrivals_two_kernel(tc, query, keys_words, keys_scales, notes_
             lo = piece * N_MM
             part, at = divmod(lo, U // 2)
             score(b, "b", piece, note_code[part][:, at : at + N_MM].bitcast(FP8X4),
-                  note_scale[:, lo : lo + N_MM])
+                  note_scale[:, lo : lo + N_MM], piece % 2 == 0)
         b_at = keep.tile([P, SLOTS], F32, name="b_at")
-        nc.scalar.activation(b_at[:, :HALF], b[:].indirect(entries(idx2, 0, HALF)), COPY)
-        nc.vector.tensor_copy(b_at[:, HALF:], b[:].indirect(entries(idx2, HALF, SLOTS)))
+        nc.vector.tensor_copy(b_at[:], b[:].indirect(idx2[:]))
 
         a = keep.tile([P, T], F32, name="a")
         for piece in range(T // N_MM):
             lo = piece * N_MM
             score(a, "a", piece, key_code[:, 2 * lo : 2 * (lo + N_MM)].bitcast(FP4X4),
-                  key_scale[:, lo : lo + N_MM])
+                  key_scale[:, lo : lo + N_MM], True)
 
         r = keep.tile([P, SLOTS], F32, name="r")
         a_at = keep.tile([P, HALF], F32, name="a_at")
@@ -109,12 +107,11 @@ def tile_attend_slotrivals_two_kernel(tc, query, keys_words, keys_scales, notes_
 
         v = keep.tile([P, SLOTS], F32, name="v")
         m1 = keep.tile([P, SLOTS], F32, name="m1")
-        nc.vector.tensor_copy(v[:, :LEAD], r[:].indirect(entries(idx3, 0, LEAD)))
-        nc.scalar.activation(v[:, LEAD:HALF], r[:].indirect(entries(idx3, LEAD, HALF)), COPY)
+        nc.vector.tensor_copy(v[:, :HALF], r[:].indirect(entries(idx3, 0, HALF)))
         nc.scalar.activation(v[:, HALF:], r[:].indirect(entries(idx3, HALF, SLOTS)), COPY)
-        for lo, hi in ((0, LEAD), (LEAD, SLOTS)):
+        for lo, hi in ((0, HALF), (HALF, SLOTS)):
             nc.vector.tensor_tensor(m1[:, lo:hi], r[:, lo:hi], v[:, lo:hi], MAX)
-            nc.vector.tensor_copy(f1[:].indirect(entries(idx4, lo, hi)), m1[:, lo:hi])
+        nc.vector.tensor_copy(f1[:].indirect(idx4[:]), m1[:])
 
         aa = keep.tile([P, T], F32, name="aa")
         nc.vector.tensor_tensor(aa[:], a[:], f1[:], SUB)

@@ -20,6 +20,8 @@ PACK = 4
 D, T, U, SLOTS, Q = 512, 1024, 1024, 512, 128
 GROUP = 16
 N_MM = 256
+PIECES = ((0, 256), (256, 512), (512, 768), (768, 896), (896, 1024))
+BANKS = 8
 HALF = SLOTS // 2
 
 FLOPS = 2 * D * Q * (T + U)
@@ -45,8 +47,9 @@ def tile_attend_slotrivals_two_kernel(tc, query, keys_words, keys_scales, notes_
         q_raw = keep.tile([P, PACK, Q], F32, name="q_raw")
         nc.sync.dma_start(out=q_raw[:], in_=query.rearrange("(p j) q -> p j q", j=PACK))
         for quad in range(4):
-            nc.sync.dma_start(out=note_scale[32 * quad : 32 * quad + 4, :].bitcast(I32),
-                                in_=notes_scales[0, 4 * quad : 4 * quad + 4, :].bitcast(I32))
+            queue = nc.sync if quad < 2 else nc.scalar
+            queue.dma_start(out=note_scale[32 * quad : 32 * quad + 4, :].bitcast(I32),
+                            in_=notes_scales[0, 4 * quad : 4 * quad + 4, :].bitcast(I32))
         note_bytes = notes_words[0].rearrange("p c r -> p (c r)")
         note_code = []
         for h in range(2):
@@ -74,30 +77,29 @@ def tile_attend_slotrivals_two_kernel(tc, query, keys_words, keys_scales, notes_
         nc.vector.quantize_mx(out=q_code[:].bitcast(FP8X4), scales=q_scale[:],
                               in_=q_bf[:].rearrange("p q j -> p (q j)"))
 
-        def score(dst, name, piece, codes, scales, on_scalar):
-            bank = psum.tile([P, N_MM], F32, name=f"{name}_bank{piece}")
+        def score(dst, bank_no, lo, hi, codes, scales, on_scalar):
+            bank = psum.tile([P, hi - lo], F32, name=f"bank{bank_no % BANKS}")
             nc.tensor.matmul_mx(out=bank[:], lhsT=q_code[:].bitcast(FP8X4), lhsT_scale=q_scale[:],
-                                rhs=codes, rhs_scale=scales, start=True, stop=True)
-            cols = dst[:, piece * N_MM : (piece + 1) * N_MM]
+                                rhs=codes, rhs_scale=scales[:, lo:hi], start=True, stop=True)
             if on_scalar:
-                nc.scalar.activation(cols, bank[:], COPY)
+                nc.scalar.activation(dst[:, lo:hi], bank[:], COPY)
             else:
-                nc.vector.tensor_copy(cols, bank[:])
+                nc.vector.tensor_copy(dst[:, lo:hi], bank[:])
+            return bank
 
         b = keep.tile([P, U], F32, name="b")
-        for piece in range(U // N_MM):
-            lo = piece * N_MM
+        for piece, (lo, hi) in enumerate(PIECES):
             part, at = divmod(lo, U // 2)
-            score(b, "b", piece, note_code[part][:, at : at + N_MM].bitcast(FP8X4),
-                  note_scale[:, lo : lo + N_MM], piece % 2 == 0)
+            score(b, piece, lo, hi, note_code[part][:, at : at + hi - lo].bitcast(FP8X4),
+                  note_scale, piece % 2 == 0)
         b_at = keep.tile([P, SLOTS], F32, name="b_at")
         nc.vector.tensor_copy(b_at[:], b[:].indirect(idx2[:]))
 
         a = keep.tile([P, T], F32, name="a")
-        for piece in range(T // N_MM):
-            lo = piece * N_MM
-            score(a, "a", piece, key_code[:, 2 * lo : 2 * (lo + N_MM)].bitcast(FP4X4),
-                  key_scale[:, lo : lo + N_MM], True)
+        a_banks = []
+        for piece, (lo, hi) in enumerate(PIECES):
+            a_banks.append(score(a, len(PIECES) + piece, lo, hi,
+                                 key_code[:, 2 * lo : 2 * hi].bitcast(FP4X4), key_scale, True))
 
         r = keep.tile([P, SLOTS], F32, name="r")
         a_at = keep.tile([P, HALF], F32, name="a_at")
@@ -114,7 +116,11 @@ def tile_attend_slotrivals_two_kernel(tc, query, keys_words, keys_scales, notes_
         nc.vector.tensor_copy(f1[:].indirect(idx4[:]), m1[:])
 
         aa = keep.tile([P, T], F32, name="aa")
-        nc.vector.tensor_tensor(aa[:], a[:], f1[:], SUB)
+        last = T - N_MM
+        nc.gpsimd.tensor_tensor(aa[:, last:], a[:, last:], f1[:, last:], SUB)
+        for piece, bank in enumerate(a_banks[:3]):
+            cols = slice(piece * N_MM, (piece + 1) * N_MM)
+            nc.vector.tensor_tensor(aa[:, cols], bank[:], f1[:, cols], SUB)
 
         res = keep.tile([P, SLOTS], F32, name="res")
         aa_at = keep.tile([P, HALF], F32, name="aa_at")

@@ -17,14 +17,24 @@ MAX = mybir.AluOpType.max
 
 P = 128
 PACK = 4
-D, T, U, SLOTS, Q = 512, 1024, 1024, 512, 128
-GROUP = 16
-N_MM = 256
-PIECES = ((0, 256), (256, 512), (512, 768), (768, 896), (896, 1024))
-BANKS = 8
+D, Q = 512, 128
+COLS = 1024
+SLOTS = 512
 HALF = SLOTS // 2
+HEAD = 16
+QUADRANTS = 4
+SCALE_ROWS = 4
+BANKS = 8
 
-FLOPS = 2 * D * Q * (T + U)
+PIECES = ((0, 256), (256, 512), (512, 768), (768, 896), (896, COLS))
+
+V_FIRST, V_SECOND, V_SCALAR = (0, 192), (192, 320), (320, SLOTS)
+
+AA_SPLIT = 704
+
+TAIL = 128
+
+FLOPS = 2 * D * Q * 2 * COLS
 
 
 def tile_attend_slotrivals_two_kernel(tc, query, keys_words, keys_scales, notes_words, notes_scales,
@@ -35,47 +45,49 @@ def tile_attend_slotrivals_two_kernel(tc, query, keys_words, keys_scales, notes_
         psum = ctx.enter_context(tc.psum_pool(name="psum", bufs=1))
 
         def entries(lst, lo, hi):
-            return lst[:, lo // GROUP : hi // GROUP]
+            return lst[:, lo // HEAD : hi // HEAD]
 
-        note_scale = keep.tile([P, U], U8, name="note_scale", align_bytes=64)
-        key_scale = keep.tile([P, T], U8, name="key_scale", align_bytes=64)
-        f1 = keep.tile([P, T], F32, name="f1")
+        def load_scales(queue, tile, scales, quad):
+            queue.dma_start(out=tile[32 * quad : 32 * quad + SCALE_ROWS, :].bitcast(I32),
+                            in_=scales[0, SCALE_ROWS * quad : SCALE_ROWS * (quad + 1), :].bitcast(I32))
+
+        note_scale = keep.tile([P, COLS], U8, name="note_scale", align_bytes=64)
+        key_scale = keep.tile([P, COLS], U8, name="key_scale", align_bytes=64)
+        f1 = keep.tile([P, COLS], F32, name="f1")
         nc.vector.memset(note_scale[:].bitcast(I32), 0)
         nc.vector.memset(key_scale[:].bitcast(I32), 0)
         nc.vector.memset(f1[:], 0.0)
 
         q_raw = keep.tile([P, PACK, Q], F32, name="q_raw")
-        nc.sync.dma_start(out=q_raw[:], in_=query.rearrange("(p j) q -> p j q", j=PACK))
-        for quad in range(4):
-            queue = nc.sync if quad < 2 else nc.scalar
-            queue.dma_start(out=note_scale[32 * quad : 32 * quad + 4, :].bitcast(I32),
-                            in_=notes_scales[0, 4 * quad : 4 * quad + 4, :].bitcast(I32))
-        note_bytes = notes_words[0].rearrange("p c r -> p (c r)")
+        nc.sync.dma_start(out=q_raw[:], in_=query.rearrange("(p t) q -> p t q", t=PACK))
+        for quad in range(QUADRANTS):
+            load_scales(nc.sync if quad < QUADRANTS // 2 else nc.scalar, note_scale, notes_scales, quad)
+        note_bytes = notes_words[0].rearrange("p c t -> p (c t)")
+        half_cols = COLS // 2
         note_code = []
         for h in range(2):
-            part = keep.tile([P, U // 2], U32, name=f"note_code{h}", align_bytes=64)
+            part = keep.tile([P, half_cols], U32, name=f"note_code{h}", align_bytes=64)
             nc.sync.dma_start(out=part[:].bitcast(I32),
-                              in_=note_bytes[:, h * 2 * U : (h + 1) * 2 * U].bitcast(I32))
+                              in_=note_bytes[:, h * half_cols * PACK : (h + 1) * half_cols * PACK].bitcast(I32))
             note_code.append(part)
-        key_code = keep.tile([P, 2 * T], U8, name="key_code", align_bytes=64)
+        key_code = keep.tile([P, 2 * COLS], U8, name="key_code", align_bytes=64)
         nc.sync.dma_start(out=key_code[:].bitcast(I32), in_=keys_words[0].bitcast(I32))
-        for quad in range(4):
-            nc.sync.dma_start(out=key_scale[32 * quad : 32 * quad + 4, :].bitcast(I32),
-                              in_=keys_scales[0, 4 * quad : 4 * quad + 4, :].bitcast(I32))
+        for quad in range(QUADRANTS):
+            load_scales(nc.sync, key_scale, keys_scales, quad)
         lists = []
         for name, src in (("idx2", offs2), ("idx", offs), ("idx3", offs3), ("idx4", offs4), ("idx5", offs5)):
-            lst = keep.tile([P, SLOTS // GROUP], U16, name=name)
+            lst = keep.tile([P, SLOTS // HEAD], U16, name=name)
             nc.sync.dma_start(lst[:], src)
             lists.append(lst)
         idx2, idx, idx3, idx4, idx5 = lists
 
         q_bf = keep.tile([P, Q, PACK], BF16, name="q_bf", align_bytes=64)
-        nc.vector.tensor_copy(out=q_bf[:].rearrange("p (c i) j -> p c j i", i=4),
-                              in_=q_raw[:].rearrange("p j (c i) -> p c j i", i=4))
+        nc.vector.tensor_copy(out=q_bf[:].rearrange("p (c i) t -> p c t i", i=4),
+                              in_=q_raw[:].rearrange("p t (c i) -> p c t i", i=4))
         q_code = keep.tile([P, Q], U32, name="q_code", align_bytes=64)
         q_scale = keep.tile([P, Q], U8, name="q_scale", align_bytes=64)
         nc.vector.quantize_mx(out=q_code[:].bitcast(FP8X4), scales=q_scale[:],
-                              in_=q_bf[:].rearrange("p q j -> p (q j)"))
+                              in_=q_bf[:].rearrange("p q t -> p (q t)"))
 
         def score(dst, bank_no, lo, hi, codes, scales, on_scalar):
             bank = psum.tile([P, hi - lo], F32, name=f"bank{bank_no % BANKS}")
@@ -87,15 +99,15 @@ def tile_attend_slotrivals_two_kernel(tc, query, keys_words, keys_scales, notes_
                 nc.vector.tensor_copy(dst[:, lo:hi], bank[:])
             return bank
 
-        b = keep.tile([P, U], F32, name="b")
+        b = keep.tile([P, COLS], F32, name="b")
         for piece, (lo, hi) in enumerate(PIECES):
-            part, at = divmod(lo, U // 2)
-            score(b, piece, lo, hi, note_code[part][:, at : at + hi - lo].bitcast(FP8X4),
+            h, at = divmod(lo, half_cols)
+            score(b, piece, lo, hi, note_code[h][:, at : at + hi - lo].bitcast(FP8X4),
                   note_scale, piece % 2 == 0)
         b_at = keep.tile([P, SLOTS], F32, name="b_at")
         nc.vector.tensor_copy(b_at[:], b[:].indirect(idx2[:]))
 
-        a = keep.tile([P, T], F32, name="a")
+        a = keep.tile([P, COLS], F32, name="a")
         a_banks = []
         for piece, (lo, hi) in enumerate(PIECES):
             a_banks.append(score(a, len(PIECES) + piece, lo, hi,
@@ -109,23 +121,27 @@ def tile_attend_slotrivals_two_kernel(tc, query, keys_words, keys_scales, notes_
 
         v = keep.tile([P, SLOTS], F32, name="v")
         m1 = keep.tile([P, SLOTS], F32, name="m1")
-        nc.vector.tensor_copy(v[:, :HALF], r[:].indirect(entries(idx3, 0, HALF)))
-        nc.scalar.activation(v[:, HALF:], r[:].indirect(entries(idx3, HALF, SLOTS)), COPY)
-        for lo, hi in ((0, HALF), (HALF, SLOTS)):
+        for lo, hi in (V_FIRST, V_SECOND):
+            nc.vector.tensor_copy(v[:, lo:hi], r[:].indirect(entries(idx3, lo, hi)))
+        lo, hi = V_SCALAR
+        nc.scalar.activation(v[:, lo:hi], r[:].indirect(entries(idx3, lo, hi)), COPY)
+        for lo, hi in (V_FIRST, V_SCALAR, V_SECOND):
             nc.vector.tensor_tensor(m1[:, lo:hi], r[:, lo:hi], v[:, lo:hi], MAX)
         nc.vector.tensor_copy(f1[:].indirect(idx4[:]), m1[:])
 
-        aa = keep.tile([P, T], F32, name="aa")
-        last = T - N_MM
-        nc.gpsimd.tensor_tensor(aa[:, last:], a[:, last:], f1[:, last:], SUB)
-        for piece, bank in enumerate(a_banks[:3]):
-            cols = slice(piece * N_MM, (piece + 1) * N_MM)
-            nc.vector.tensor_tensor(aa[:, cols], bank[:], f1[:, cols], SUB)
+        aa = keep.tile([P, COLS], F32, name="aa")
+        nc.gpsimd.tensor_tensor(aa[:, AA_SPLIT:], a[:, AA_SPLIT:], f1[:, AA_SPLIT:], SUB)
+        for (lo, hi), bank in zip(PIECES, a_banks):
+            hi = min(hi, AA_SPLIT)
+            if lo < hi:
+                nc.vector.tensor_tensor(aa[:, lo:hi], bank[:, : hi - lo], f1[:, lo:hi], SUB)
 
         res = keep.tile([P, SLOTS], F32, name="res")
         aa_at = keep.tile([P, HALF], F32, name="aa_at")
         nc.vector.tensor_tensor(res[:, :HALF], aa[:].indirect(entries(idx5, 0, HALF)), v[:, :HALF], ADD)
         nc.scalar.activation(aa_at[:], aa[:].indirect(entries(idx5, HALF, SLOTS)), COPY)
         nc.sync.dma_start(out=out[:, :HALF], in_=res[:, :HALF])
-        nc.vector.tensor_tensor(res[:, HALF:], aa_at[:], v[:, HALF:], ADD)
-        nc.sync.dma_start(out=out[:, HALF:], in_=res[:, HALF:])
+        for lo in range(HALF, SLOTS, TAIL):
+            cols = slice(lo, lo + TAIL)
+            nc.vector.tensor_tensor(res[:, cols], aa_at[:, lo - HALF : lo - HALF + TAIL], v[:, cols], ADD)
+            nc.sync.dma_start(out=out[:, cols], in_=res[:, cols])

from contextlib import ExitStack

import concourse.mybir as mybir

F32 = mybir.dt.float32
BF16 = mybir.dt.bfloat16
I32 = mybir.dt.int32
U32 = mybir.dt.uint32
U16 = mybir.dt.uint16
U8 = mybir.dt.uint8
FP8X4 = mybir.dt.float8_e4m3fn_x4
FP4X4 = mybir.dt.float4_e2m1fn_x4
COPY = mybir.ActivationFunctionType.Copy
ADD = mybir.AluOpType.add
SUB = mybir.AluOpType.subtract
MAX = mybir.AluOpType.max

P = 128
PACK = 4
D, Q = 512, 128
COLS = 1024
SLOTS = 512
HALF = SLOTS // 2
HEAD = 16
QUADRANTS = 4
SCALE_ROWS = 4
BANKS = 8

PIECES = ((0, 256), (256, 512), (512, 768), (768, 896), (896, COLS))

V_FIRST, V_SECOND, V_SCALAR = (0, 192), (192, 320), (320, SLOTS)

AA_SPLIT = 704

TAIL = 128

FLOPS = 2 * D * Q * 2 * COLS


def tile_attend_slotrivals_two_kernel(tc, query, keys_words, keys_scales, notes_words, notes_scales,
                                       offs, offs2, offs3, offs4, offs5, out):
    nc = tc.nc
    with ExitStack() as ctx:
        keep = ctx.enter_context(tc.tile_pool(name="keep", bufs=1))
        psum = ctx.enter_context(tc.psum_pool(name="psum", bufs=1))

        def entries(lst, lo, hi):
            return lst[:, lo // HEAD : hi // HEAD]

        def load_scales(queue, tile, scales, quad):
            queue.dma_start(out=tile[32 * quad : 32 * quad + SCALE_ROWS, :].bitcast(I32),
                            in_=scales[0, SCALE_ROWS * quad : SCALE_ROWS * (quad + 1), :].bitcast(I32))

        note_scale = keep.tile([P, COLS], U8, name="note_scale", align_bytes=64)
        key_scale = keep.tile([P, COLS], U8, name="key_scale", align_bytes=64)
        f1 = keep.tile([P, COLS], F32, name="f1")
        nc.vector.memset(note_scale[:].bitcast(I32), 0)
        nc.vector.memset(key_scale[:].bitcast(I32), 0)
        nc.vector.memset(f1[:], 0.0)

        q_raw = keep.tile([P, PACK, Q], F32, name="q_raw")
        nc.sync.dma_start(out=q_raw[:], in_=query.rearrange("(p t) q -> p t q", t=PACK))
        for quad in range(QUADRANTS):
            load_scales(nc.sync if quad < QUADRANTS // 2 else nc.scalar, note_scale, notes_scales, quad)
        note_bytes = notes_words[0].rearrange("p c t -> p (c t)")
        half_cols = COLS // 2
        note_code = []
        for h in range(2):
            part = keep.tile([P, half_cols], U32, name=f"note_code{h}", align_bytes=64)
            nc.sync.dma_start(out=part[:].bitcast(I32),
                              in_=note_bytes[:, h * half_cols * PACK : (h + 1) * half_cols * PACK].bitcast(I32))
            note_code.append(part)
        key_code = keep.tile([P, 2 * COLS], U8, name="key_code", align_bytes=64)
        nc.sync.dma_start(out=key_code[:].bitcast(I32), in_=keys_words[0].bitcast(I32))
        for quad in range(QUADRANTS):
            load_scales(nc.sync, key_scale, keys_scales, quad)
        lists = []
        for name, src in (("idx2", offs2), ("idx", offs), ("idx3", offs3), ("idx4", offs4), ("idx5", offs5)):
            lst = keep.tile([P, SLOTS // HEAD], U16, name=name)
            nc.sync.dma_start(lst[:], src)
            lists.append(lst)
        idx2, idx, idx3, idx4, idx5 = lists

        q_bf = keep.tile([P, Q, PACK], BF16, name="q_bf", align_bytes=64)
        nc.vector.tensor_copy(out=q_bf[:].rearrange("p (c i) t -> p c t i", i=4),
                              in_=q_raw[:].rearrange("p t (c i) -> p c t i", i=4))
        q_code = keep.tile([P, Q], U32, name="q_code", align_bytes=64)
        q_scale = keep.tile([P, Q], U8, name="q_scale", align_bytes=64)
        nc.vector.quantize_mx(out=q_code[:].bitcast(FP8X4), scales=q_scale[:],
                              in_=q_bf[:].rearrange("p q t -> p (q t)"))

        def score(dst, bank_no, lo, hi, codes, scales, on_scalar):
            bank = psum.tile([P, hi - lo], F32, name=f"bank{bank_no % BANKS}")
            nc.tensor.matmul_mx(out=bank[:], lhsT=q_code[:].bitcast(FP8X4), lhsT_scale=q_scale[:],
                                rhs=codes, rhs_scale=scales[:, lo:hi], start=True, stop=True)
            if on_scalar:
                nc.scalar.activation(dst[:, lo:hi], bank[:], COPY)
            else:
                nc.vector.tensor_copy(dst[:, lo:hi], bank[:])
            return bank

        b = keep.tile([P, COLS], F32, name="b")
        for piece, (lo, hi) in enumerate(PIECES):
            h, at = divmod(lo, half_cols)
            score(b, piece, lo, hi, note_code[h][:, at : at + hi - lo].bitcast(FP8X4),
                  note_scale, piece % 2 == 0)
        b_at = keep.tile([P, SLOTS], F32, name="b_at")
        nc.vector.tensor_copy(b_at[:], b[:].indirect(idx2[:]))

        a = keep.tile([P, COLS], F32, name="a")
        a_banks = []
        for piece, (lo, hi) in enumerate(PIECES):
            a_banks.append(score(a, len(PIECES) + piece, lo, hi,
                                 key_code[:, 2 * lo : 2 * hi].bitcast(FP4X4), key_scale, True))

        r = keep.tile([P, SLOTS], F32, name="r")
        a_at = keep.tile([P, HALF], F32, name="a_at")
        nc.vector.tensor_tensor(r[:, :HALF], a[:].indirect(entries(idx, 0, HALF)), b_at[:, :HALF], SUB)
        nc.scalar.activation(a_at[:], a[:].indirect(entries(idx, HALF, SLOTS)), COPY)
        nc.vector.tensor_tensor(r[:, HALF:], a_at[:], b_at[:, HALF:], SUB)

        v = keep.tile([P, SLOTS], F32, name="v")
        m1 = keep.tile([P, SLOTS], F32, name="m1")
        for lo, hi in (V_FIRST, V_SECOND):
            nc.vector.tensor_copy(v[:, lo:hi], r[:].indirect(entries(idx3, lo, hi)))
        lo, hi = V_SCALAR
        nc.scalar.activation(v[:, lo:hi], r[:].indirect(entries(idx3, lo, hi)), COPY)
        for lo, hi in (V_FIRST, V_SCALAR, V_SECOND):
            nc.vector.tensor_tensor(m1[:, lo:hi], r[:, lo:hi], v[:, lo:hi], MAX)
        nc.vector.tensor_copy(f1[:].indirect(idx4[:]), m1[:])

        aa = keep.tile([P, COLS], F32, name="aa")
        nc.gpsimd.tensor_tensor(aa[:, AA_SPLIT:], a[:, AA_SPLIT:], f1[:, AA_SPLIT:], SUB)
        for (lo, hi), bank in zip(PIECES, a_banks):
            hi = min(hi, AA_SPLIT)
            if lo < hi:
                nc.vector.tensor_tensor(aa[:, lo:hi], bank[:, : hi - lo], f1[:, lo:hi], SUB)

        res = keep.tile([P, SLOTS], F32, name="res")
        aa_at = keep.tile([P, HALF], F32, name="aa_at")
        nc.vector.tensor_tensor(res[:, :HALF], aa[:].indirect(entries(idx5, 0, HALF)), v[:, :HALF], ADD)
        nc.scalar.activation(aa_at[:], aa[:].indirect(entries(idx5, HALF, SLOTS)), COPY)
        nc.sync.dma_start(out=out[:, :HALF], in_=res[:, :HALF])
        for lo in range(HALF, SLOTS, TAIL):
            cols = slice(lo, lo + TAIL)
            nc.vector.tensor_tensor(res[:, cols], aa_at[:, lo - HALF : lo - HALF + TAIL], v[:, cols], ADD)
            nc.sync.dma_start(out=out[:, cols], in_=res[:, cols])
